import numpy as np
import ml_dtypes


def mxq(x, axis, fmt="e4m3"):
    dtype, down = {"e4m3": (ml_dtypes.float8_e4m3fn, 7), "e5m2": (ml_dtypes.float8_e5m2, 14)}[fmt]
    v = np.moveaxis(np.asarray(x, np.float32).astype(ml_dtypes.bfloat16).astype(np.float64), axis, -1)
    blocks = v.reshape(v.shape[:-1] + (-1, 32))
    amax = np.abs(blocks).max(-1, keepdims=True)
    byte = np.maximum(np.where(amax > 0, np.frexp(amax)[1] - 1 + 127, 0) - down, 1)
    scale = np.exp2(byte - 127.0)
    codes = (blocks / scale).astype(np.float32).astype(dtype).astype(np.float64)
    return np.moveaxis((codes * scale).reshape(v.shape), -1, axis)


WIDE = False


def mx_kscale(k):
    if not WIDE:
        return np.ones(k)
    levels = np.array([10, -10, 5, -5, 0])
    if k % 512:
        return np.exp2(np.random.permutation(np.resize(levels, k // 32))).repeat(32)
    a = np.empty((k // 512, 16))
    for p in range(k // 512):
        a[p, :8] = np.random.permutation(np.resize(levels, 8))
        for g in range(8):
            far = levels[np.abs(levels - a[p, g]) >= 10]
            a[p, g + 8] = far[np.random.randint(len(far))]
    return np.exp2(a.ravel()).repeat(32)


def f64(x):
    return np.asarray(x).astype(np.float64)


def striped(idx):
    return np.tile(idx.reshape(-1, 16).T, (8, 1)).astype(np.uint16)


def unstriped(offs):
    return offs[:16].T.reshape(-1).astype(np.int64)


E2M1 = np.array([0.0, 0.5, 1.0, 1.5, 2.0, 3.0, 4.0, 6.0, -0.0, -0.5, -1.0, -1.5, -2.0, -3.0, -4.0, -6.0])


def pack_weight(w, fmt):
    k, n = w.shape
    w = f64(np.asarray(w, np.float32).astype(ml_dtypes.bfloat16)).reshape(k // 32, 32, n)
    amax = np.abs(w).max(1)
    if fmt == "e4m3":
        byte = np.frexp(amax)[1] - 1 + 127 - 7
    else:
        mant, ex = np.frexp(amax / 6.0)
        byte = np.where(mant > 0.5, ex, ex - 1) + 127
    byte = np.clip(np.where(amax > 0, byte, 1), 1, 254)
    scaled = (w * np.exp2(127.0 - byte)[:, None, :]).reshape(k, n).astype(np.float32)
    by_word = np.ascontiguousarray(scaled.reshape(k // 512, 128, 4, n).transpose(0, 1, 3, 2))
    if fmt == "e4m3":
        words = by_word.astype(ml_dtypes.float8_e4m3fn).view(np.uint8)
    else:
        c = by_word.astype(ml_dtypes.float4_e2m1fn).view(np.uint8) & 0xF
        words = (c[..., 0::2] | (c[..., 1::2] << 4)).reshape(k // 512, 128, 2 * n)
    return np.ascontiguousarray(words), np.ascontiguousarray(byte.astype(np.uint8).reshape(k // 512, 16, n))


def unpack_weight(words, scales, fmt):
    g, _, n = scales.shape
    words = np.ascontiguousarray(words).reshape(g, 128, n, -1)
    if fmt == "e4m3":
        vals = words.view(ml_dtypes.float8_e4m3fn).astype(np.float64)
    else:
        nib = np.empty((g, 128, n, 4), np.uint8)
        nib[..., 0::2] = words & 0xF
        nib[..., 1::2] = words >> 4
        vals = E2M1[nib]
    vals = vals * np.repeat(np.exp2(scales.astype(np.float64) - 127.0), 8, axis=1)[..., None]
    return vals.transpose(0, 1, 3, 2).reshape(g * 512, n)


def gelu(v):
    return 0.5 * v * (1.0 + np.tanh(np.sqrt(2.0 / np.pi) * (v + 0.044715 * v**3)))


K, T, S, P, H, N = 1024, 4096, 1024, 512, 1024, 768

def setup_inputs():
    n = np.random.standard_normal
    s = mx_kscale(K)[:, None]
    u = mx_kscale(H)[:, None]
    perm = np.random.permutation(S)
    tab_words, tab_scales = pack_weight(n((K, T)) * s, "e4m3")
    w4_words, w4_scales = pack_weight(0.72 * n((K, H)) / np.sqrt(K) / s, "e2m1")
    return {
        "tab_words": tab_words, "tab_scales": tab_scales,
        "offs": striped(np.random.permutation(T)[:S]),
        "pos1": striped(perm[:P]),
        "pos2": striped(perm[P:]),
        "w4_words": w4_words, "w4_scales": w4_scales,
        "dens": np.random.uniform(0.6, 1.4, (H, S)).astype(np.float32),
        "temp": np.random.uniform(0.4, 1.6, H).astype(np.float32),
        "tint": (np.sign(n(H)) * np.random.uniform(2.0, 7.0, H)).astype(np.float32),
        "skip": (1.6 * np.exp(0.3 * n(H))).astype(np.float32),
        "wgs": np.exp(0.3 * n((128, P))).astype(np.float32),
        "gain": (np.random.uniform(0.6, 1.8, H) * u[:, 0]).astype(np.float32),
        "w2": (1.2 * n((H, N)) / np.sqrt(H) / u).astype(np.float32),
    }

def reference(tab_words, tab_scales, offs, pos1, pos2, w4_words, w4_scales, dens, temp, tint, skip, wgs, gain, w2):
    v = unpack_weight(tab_words, tab_scales, "e4m3")[:, unstriped(offs)]
    w4 = unpack_weight(w4_words, w4_scales, "e2m1")
    h = (w4.T @ v) * f64(dens)
    top = h.max(axis=1)
    a = np.exp(f64(temp)[:, None] * (h[:, unstriped(pos1)] - top[:, None]))
    a = f64(tint)[:, None] * a
    page = f64(skip)[:, None] * h
    page[:, unstriped(pos2)] = np.tile(f64(wgs), (H // 128, 1)) * a
    f = mxq(f64(gain)[:, None] * np.tanh(page), 0, "e4m3")
    return np.abs(mxq(f64(w2), 0, "e4m3").T @ f)

@@ -1,0 +1,262 @@
+from contextlib import ExitStack
+
+import concourse.mybir as mybir
+from concourse.masks import make_identity
+
+K, T, S, NP, H, N = 1024, 4096, 1024, 512, 1024, 768
+FLOPS = 2 * K * H * S + 2 * H * N * S
+
+F32 = mybir.dt.float32
+BF16 = mybir.dt.bfloat16
+I32 = mybir.dt.int32
+U32 = mybir.dt.uint32
+U16 = mybir.dt.uint16
+U8 = mybir.dt.uint8
+FP8X4 = mybir.dt.float8_e4m3fn_x4
+FP4X4 = mybir.dt.float4_e2m1fn_x4
+ACT = mybir.ActivationFunctionType
+ALU = mybir.AluOpType
+AX = mybir.AxisListType
+
+P = 128
+PACK = 4
+PASSES = 2
+TILES = PASSES * PACK
+BANK = 512
+CHUNK = 256
+W2_PIECE = 384
+
+
+def tile_list_slide_dye_repair_kernel(tc, tab_words, tab_scales, offs, pos1, pos2, w4_words, w4_scales,
+                                                dens, temp, tint, skip, wgs, gain, w2, out):
+    nc = tc.nc
+    with ExitStack() as ctx:
+        keep = ctx.enter_context(tc.tile_pool(name="keep", bufs=1))
+        ring = ctx.enter_context(tc.tile_pool(name="ring", bufs=2))
+        psum = ctx.enter_context(tc.psum_pool(name="psum", bufs=4))
+
+        def kept(shape, dtype, name):
+            return keep.tile(shape, dtype, name=name, align_bytes=64)
+
+        idx = keep.tile([P, S // 16], U16, name="idx")
+        nc.sync.dma_start(idx[:], offs)
+        table = [kept([P, T], I32, "table%d" % a) for a in range(PASSES)]
+        for a in range(PASSES):
+            nc.sync.dma_start(table[a][:], tab_words[a].rearrange("p t i -> p (t i)").bitcast(I32))
+
+        table_scales = kept([P, T], U8, "table_scales")
+        nc.scalar.dma_start(table_scales[0:32, :].bitcast(I32), tab_scales.rearrange("a r t -> r a t").bitcast(I32))
+        wgs_rows = kept([P, NP], F32, "wgs_rows")
+        nc.scalar.dma_start(wgs_rows[:], wgs)
+        rowvec = {}
+
+        def load_rowvec(queue, name, vec):
+            rowvec[name] = kept([P, TILES], F32, name + "_rows")
+            queue.dma_start(rowvec[name][:].rearrange("p (b t) -> p b t", t=PACK),
+                            vec.rearrange("(b p t) -> p b t", p=P, t=PACK))
+
+        load_rowvec(nc.scalar, "tint", tint)
+
+        ident = kept([P, P], F32, "ident")
+        make_identity(nc, ident[:])
+        w4s_raw = kept([P, PASSES, H], U8, "w4s_raw")
+        nc.vector.memset(w4s_raw[:].bitcast(I32), 0)
+        v_scales = kept([P, PASSES, S], U8, "v_scales")
+        nc.vector.memset(v_scales[:].bitcast(I32), 0)
+        for q in range(4):
+            nc.gpsimd.dma_start(w4s_raw[32 * q : 32 * q + 4].bitcast(I32),
+                                w4_scales[:, 4 * q : 4 * q + 4, :].rearrange("a r c -> r a c").bitcast(I32))
+        nc.vector.memset(table_scales[32:64, :].bitcast(I32), 0)
+        nc.vector.memset(table_scales[64:P, :].bitcast(I32), 0)
+
+        w4_raw = [kept([P, PASSES, BANK], U16, "w4_raw%d" % b) for b in range(PASSES)]
+
+        def load_w4(b):
+            nc.sync.dma_start(w4_raw[b][:].bitcast(I32),
+                              w4_words[:, :, 2 * BANK * b : 2 * BANK * (b + 1)].rearrange("a p c -> p a c").bitcast(I32))
+
+        dens_rows = dens.rearrange("(b p t) j -> b t p j", p=P, t=PACK)
+        dens_sb = {}
+
+        def load_dens(i):
+            dens_sb[i] = ring.tile([P, S], F32, name="dens_sb", bufs=6)
+            nc.sync.dma_start(dens_sb[i][:], dens_rows[i // PACK, i % PACK])
+
+        load_w4(0)
+        load_dens(0)
+        p1 = keep.tile([P, NP // 16], U16, name="p1")
+        nc.sync.dma_start(p1[:], pos1)
+        p2 = keep.tile([P, NP // 16], U16, name="p2")
+        nc.sync.dma_start(p2[:], pos2)
+        load_rowvec(nc.sync, "temp", temp)
+        load_rowvec(nc.sync, "skip", skip)
+        load_rowvec(nc.sync, "gain", gain)
+        load_dens(1)
+        load_dens(2)
+        load_w4(1)
+        load_dens(3)
+        w2_raw = [kept([P, PACK, N], F32, "w2_raw%d" % b) for b in range(PASSES)]
+        w2_rows = w2.rearrange("(b p t) n -> b p t n", p=P, t=PACK)
+        nc.sync.dma_start(w2_raw[0][:], w2_rows[0])
+        load_dens(4)
+        load_dens(5)
+        nc.sync.dma_start(w2_raw[1][:], w2_rows[1])
+
+        picked_scales = kept([P, S], U8, "picked_scales")
+        nc.vector.tensor_copy(picked_scales[:], table_scales[:].indirect(idx[:]))
+        for q in range(4):
+            nc.gpsimd.dma_start(v_scales[32 * q : 32 * q + 4].bitcast(I32),
+                                picked_scales[8 * q : 8 * q + 8, :].bitcast(I32))
+        w4_sc = kept([P, PASSES, H], U8, "w4_sc")
+        nc.vector.tensor_copy(w4_sc[:].rearrange("p a (b t m) -> p a b t m", b=PASSES, t=PACK),
+                              w4s_raw[:].rearrange("p a (b m t) -> p a b t m", b=PASSES, t=PACK))
+
+        turned = psum.tile([P, BANK], F32, name="turned", tag="h_bank")
+        for c in range(4):
+            nc.tensor.transpose(turned[:, P * c : P * (c + 1)], wgs_rows[:, P * c : P * (c + 1)], ident[:])
+        spread = kept([P, 4, PACK, 4, 32], F32, "spread")
+        for c in range(4):
+            nc.scalar.copy(spread[:, c],
+                           turned[:, P * c : P * (c + 1)].rearrange("p (i t) -> p t i", t=PACK).unsqueeze(2).to_broadcast([P, PACK, 4, 32]))
+        weight = {}
+        for t in range(PACK):
+            dealt = psum.tile([P, BANK], F32, name="dealt", tag="aux_bank")
+            for c in range(4):
+                nc.tensor.transpose(dealt[:, P * c : P * (c + 1)], spread[:, c, t].rearrange("p q i -> p (q i)"), ident[:])
+            for b in range(PASSES):
+                i = PACK * b + t
+                weight[i] = kept([P, NP], F32, "weight%d" % i)
+                nc.scalar.activation(weight[i][:], dealt[:], ACT.Copy, scale=rowvec["tint"][:, i : i + 1])
+
+        v0 = kept([P, S], U32, "v0")
+        nc.vector.tensor_copy(v0[:], table[0][:].bitcast(U32).indirect(idx[:]))
+        v1 = [kept([P, BANK], U32, "v1_%d" % u) for u in range(2)]
+        for u in range(2):
+            nc.vector.tensor_copy(v1[u][:], table[1][:].bitcast(U32).indirect(idx[:, 32 * u : 32 * (u + 1)]))
+        w4_w = [kept([P, PASSES, BANK], U16, "w4_w%d" % b) for b in range(PASSES)]
+
+        def deal_w4(b, t0, t1):
+            nc.scalar.copy(w4_w[b][:].rearrange("p a (t m) -> p a t m", t=PACK)[:, :, t0:t1],
+                           w4_raw[b][:].rearrange("p a (m t) -> p a t m", t=PACK)[:, :, t0:t1])
+
+        top = kept([P, TILES], F32, "top")
+        look_bias = kept([P, TILES], F32, "look_bias")
+        h, page, look, bent = {}, {}, {}, {}
+        f_rows = [ring.tile([P, PACK, S], BF16, name="f_rows") for b in range(PASSES)]
+        f_codes = [kept([P, S], U32, "f_codes%d" % b) for b in range(PASSES)]
+        f_scales = [kept([P, S], U8, "f_scales%d" % b) for b in range(PASSES)]
+        w2_codes = [kept([P, N], U32, "w2_codes%d" % b) for b in range(PASSES)]
+        w2_scales = [kept([P, N], U8, "w2_scales%d" % b) for b in range(PASSES)]
+
+        def make_h(i):
+            b, t = divmod(i, PACK)
+            h[i] = ring.tile([P, S], F32, name="h", bufs=3)
+            page[i] = ring.tile([P, S], F32, name="page", bufs=3)
+            for u in range(2):
+                cols = slice(BANK * u, BANK * (u + 1))
+                bank = psum.tile([P, BANK], F32, name="bank", tag="h_bank")
+                for a in range(PASSES):
+                    nc.tensor.matmul_mx(
+                        out=bank[:],
+                        lhsT=w4_w[b][:, a, P * t : P * (t + 1)].bitcast(FP4X4),
+                        lhsT_scale=w4_sc[:, a, P * i : P * (i + 1)],
+                        rhs=(v0[:, cols] if a == 0 else v1[u][:]).bitcast(FP8X4),
+                        rhs_scale=v_scales[:, a, cols],
+                        start=(a == 0), stop=(a == PASSES - 1))
+                nc.vector.tensor_tensor(h[i][:, cols], bank[:], dens_sb[i][:, cols], ALU.mult)
+                nc.gpsimd.tensor_scalar(page[i][:, cols], h[i][:, cols], rowvec["skip"][:, i : i + 1], 0.0, ALU.mult, ALU.add)
+            nc.vector.tensor_reduce(top[:, i : i + 1], h[i][:], AX.X, ALU.max)
+
+        def look_at_h(i):
+            nc.scalar.activation(look_bias[:, i : i + 1], top[:, i : i + 1], ACT.Copy, scale=neg_temp[:, i : i + 1])
+            look[i] = ring.tile([P, NP], F32, name="look")
+            nc.scalar.activation(look[i][:], h[i][:].indirect(p1[:]), ACT.Exp,
+                                 bias=look_bias[:, i : i + 1], scale=rowvec["temp"][:, i : i + 1])
+
+        def put(i):
+            nc.vector.tensor_tensor(page[i][:].indirect(p2[:]), look[i][:], weight[i][:], ALU.mult)
+
+        def bend(i):
+            b, t = divmod(i, PACK)
+            bent[i] = ring.tile([P, S], F32, name="bent")
+            nc.scalar.activation(bent[i][:], page[i][:], ACT.Tanh)
+            nc.scalar.activation(f_rows[b][:, t], bent[i][:], ACT.Copy, scale=rowvec["gain"][:, i : i + 1])
+
+        def weave(copy, rows, width):
+            woven = ring.tile([P, width, PACK], BF16, name="woven", bufs=3, align_bytes=64)
+            copy(woven[:].rearrange("p (c i) t -> p c t i", i=4), rows.rearrange("p t (c i) -> p c t i", i=4))
+            return woven
+
+        def quantise(woven, codes, scales):
+            nc.vector.quantize_mx(out=codes.bitcast(FP8X4), scales=scales, in_=woven[:].rearrange("p w t -> p (w t)"))
+
+        def w2_piece(k):
+            b, u = divmod(k, 2)
+            cols = slice(W2_PIECE * u, W2_PIECE * (u + 1))
+            quantise(weave(nc.scalar.copy, w2_raw[b][:, :, cols], W2_PIECE), w2_codes[b][:, cols], w2_scales[b][:, cols])
+
+        def f_piece(b, c, copy):
+            cols = slice(CHUNK * c, CHUNK * (c + 1))
+            quantise(weave(copy, f_rows[b][:, :, cols], CHUNK), f_codes[b][:, cols], f_scales[b][:, cols])
+
+        def out_pass(bank, c, pair, b):
+            cols = slice(CHUNK * c, CHUNK * (c + 1))
+            for e in range(2):
+                rows = slice(P * (2 * pair + e), P * (2 * pair + e + 1))
+                nc.tensor.matmul_mx(
+                    out=bank[:, CHUNK * e : CHUNK * (e + 1)],
+                    lhsT=w2_codes[b][:, rows].bitcast(FP8X4), lhsT_scale=w2_scales[b][:, rows],
+                    rhs=f_codes[b][:, cols].bitcast(FP8X4), rhs_scale=f_scales[b][:, cols],
+                    start=(b == 0 and e == 0), stop=(b == PASSES - 1 and e == 1))
+
+        neg_temp = kept([P, TILES], F32, "neg_temp")
+        nc.scalar.activation(neg_temp[:], rowvec["temp"][:], ACT.Copy, scale=-1.0)
+        deal_w4(0, 0, 1)
+        deal_w4(0, 1, PACK)
+        make_h(0)
+        look_at_h(0)
+        for i in range(TILES):
+            if i + 6 < TILES:
+                load_dens(i + 6)
+            if i == 1:
+                deal_w4(1, 0, PACK)
+            if i + 1 < TILES:
+                make_h(i + 1)
+                look_at_h(i + 1)
+            put(i)
+            if i + 1 < TILES:
+                bend(i)
+            if i in (1, 2):
+                w2_piece(i - 1)
+            if i in (3, 4):
+                f_piece(0, 2 * (i - 3), nc.scalar.copy)
+                f_piece(0, 2 * (i - 3) + 1, nc.scalar.copy)
+            if i in (5, 6):
+                w2_piece(i - 3)
+
+        out_rows = out.rearrange("(pair e p) j -> pair p e j", e=2, p=P)
+        banks = {}
+
+        def open_bank(k):
+            banks[k] = psum.tile([P, BANK], F32, name="acc", tag=("aux_bank" if (k // 4) % 2 == 0 else "h_bank"))
+            out_pass(banks[k], k // 3, k % 3, 0)
+
+        for k in range(8):
+            open_bank(k)
+        last = TILES - 1
+        bent[last] = ring.tile([P, S], F32, name="bent")
+        for c in range(S // CHUNK):
+            cols = slice(CHUNK * c, CHUNK * (c + 1))
+            nc.scalar.activation(bent[last][:, cols], page[last][:, cols], ACT.Tanh)
+        for c in range(S // CHUNK):
+            cols = slice(CHUNK * c, CHUNK * (c + 1))
+            nc.vector.tensor_scalar(f_rows[1][:, PACK - 1, cols], bent[last][:, cols], rowvec["gain"][:, last : last + 1], None, ALU.mult)
+            f_piece(1, c, nc.vector.tensor_copy)
+            for pair in range(3):
+                k = 3 * c + pair
+                if k not in banks:
+                    open_bank(k)
+                out_pass(banks[k], c, pair, 1)
+                result = ring.tile([P, 2, CHUNK], F32, name="result", bufs=6)
+                nc.scalar.activation(result[:].rearrange("p e j -> p (e j)"), banks[k][:], ACT.Abs)
+                nc.sync.dma_start(out_rows[pair][:, :, cols], result[:])

@@ -25,6 +25,7 @@ TILES = PASSES * PACK
 BANK = 512
 CHUNK = 256
 W2_PIECE = 384
+AHEAD = 2
 
 
 def tile_list_slide_dye_repair_kernel(tc, tab_words, tab_scales, offs, pos1, pos2, w4_words, w4_scales,
@@ -40,14 +41,12 @@ def tile_list_slide_dye_repair_kernel(tc, tab_words, tab_scales, offs, pos1, pos
 
         idx = keep.tile([P, S // 16], U16, name="idx")
         nc.sync.dma_start(idx[:], offs)
-        table = [kept([P, T], I32, "table%d" % a) for a in range(PASSES)]
-        for a in range(PASSES):
-            nc.sync.dma_start(table[a][:], tab_words[a].rearrange("p t i -> p (t i)").bitcast(I32))
-
         table_scales = kept([P, T], U8, "table_scales")
-        nc.scalar.dma_start(table_scales[0:32, :].bitcast(I32), tab_scales.rearrange("a r t -> r a t").bitcast(I32))
+        w4s_raw = kept([P, H], U8, "w4s_raw")
+        nc.sync.dma_start(w4s_raw[0:32, :].bitcast(I32), w4_scales.rearrange("a r c -> r a c").bitcast(I32))
+        nc.sync.dma_start(table_scales[0:32, :].bitcast(I32), tab_scales.rearrange("a r t -> r a t").bitcast(I32))
         wgs_rows = kept([P, NP], F32, "wgs_rows")
-        nc.scalar.dma_start(wgs_rows[:], wgs)
+        nc.sync.dma_start(wgs_rows[:], wgs)
         rowvec = {}
 
         def load_rowvec(queue, name, vec):
@@ -55,19 +54,29 @@ def tile_list_slide_dye_repair_kernel(tc, tab_words, tab_scales, offs, pos1, pos
             queue.dma_start(rowvec[name][:].rearrange("p (b t) -> p b t", t=PACK),
                             vec.rearrange("(b p t) -> p b t", p=P, t=PACK))
 
-        load_rowvec(nc.scalar, "tint", tint)
+        load_rowvec(nc.sync, "tint", tint)
+        table = [kept([P, T], I32, "table%d" % a) for a in range(PASSES)]
+        for a in range(PASSES):
+            nc.sync.dma_start(table[a][:], tab_words[a].rearrange("p t i -> p (t i)").bitcast(I32))
 
         ident = kept([P, P], F32, "ident")
         make_identity(nc, ident[:])
-        w4s_raw = kept([P, PASSES, H], U8, "w4s_raw")
-        nc.vector.memset(w4s_raw[:].bitcast(I32), 0)
+        for rows in (w4s_raw, table_scales):
+            nc.vector.memset(rows[32:64, :].bitcast(I32), 0)
+            nc.vector.memset(rows[64:P, :].bitcast(I32), 0)
+        w4_sc = kept([P, PASSES, H], U8, "w4_sc")
         v_scales = kept([P, PASSES, S], U8, "v_scales")
-        nc.vector.memset(v_scales[:].bitcast(I32), 0)
-        for q in range(4):
-            nc.gpsimd.dma_start(w4s_raw[32 * q : 32 * q + 4].bitcast(I32),
-                                w4_scales[:, 4 * q : 4 * q + 4, :].rearrange("a r c -> r a c").bitcast(I32))
-        nc.vector.memset(table_scales[32:64, :].bitcast(I32), 0)
-        nc.vector.memset(table_scales[64:P, :].bitcast(I32), 0)
+        for plane in (w4_sc, v_scales):
+            nc.gpsimd.memset(plane[:].bitcast(I32), 0)
+
+        def to_planes(planes, rows):
+            for q in range(4):
+                nc.gpsimd.dma_start(planes[32 * q : 32 * q + 4].bitcast(I32), rows[8 * q : 8 * q + 8, :].bitcast(I32))
+
+        w4s_dealt = kept([P, H], U8, "w4s_dealt")
+        nc.vector.tensor_copy(w4s_dealt[:].rearrange("p (b t m) -> p b t m", b=PASSES, t=PACK),
+                              w4s_raw[:].rearrange("p (b m t) -> p b t m", b=PASSES, t=PACK))
+        to_planes(w4_sc, w4s_dealt)
 
         w4_raw = [kept([P, PASSES, BANK], U16, "w4_raw%d" % b) for b in range(PASSES)]
 
@@ -79,7 +88,7 @@ def tile_list_slide_dye_repair_kernel(tc, tab_words, tab_scales, offs, pos1, pos
         dens_sb = {}
 
         def load_dens(i):
-            dens_sb[i] = ring.tile([P, S], F32, name="dens_sb", bufs=6)
+            dens_sb[i] = ring.tile([P, S], F32, name="dens_sb", tag="stream", bufs=5)
             nc.sync.dma_start(dens_sb[i][:], dens_rows[i // PACK, i % PACK])
 
         load_w4(0)
@@ -95,21 +104,17 @@ def tile_list_slide_dye_repair_kernel(tc, tab_words, tab_scales, offs, pos1, pos
         load_dens(2)
         load_w4(1)
         load_dens(3)
-        w2_raw = [kept([P, PACK, N], F32, "w2_raw%d" % b) for b in range(PASSES)]
+        w2_raw = {}
         w2_rows = w2.rearrange("(b p t) n -> b p t n", p=P, t=PACK)
-        nc.sync.dma_start(w2_raw[0][:], w2_rows[0])
-        load_dens(4)
-        load_dens(5)
-        nc.sync.dma_start(w2_raw[1][:], w2_rows[1])
+
+        def load_w2(k):
+            b, u = divmod(k, 2)
+            w2_raw[k] = ring.tile([P, PACK, W2_PIECE], F32, name="w2_raw", tag="stream", bufs=5)
+            nc.sync.dma_start(w2_raw[k][:], w2_rows[b][:, :, W2_PIECE * u : W2_PIECE * (u + 1)])
 
         picked_scales = kept([P, S], U8, "picked_scales")
         nc.vector.tensor_copy(picked_scales[:], table_scales[:].indirect(idx[:]))
-        for q in range(4):
-            nc.gpsimd.dma_start(v_scales[32 * q : 32 * q + 4].bitcast(I32),
-                                picked_scales[8 * q : 8 * q + 8, :].bitcast(I32))
-        w4_sc = kept([P, PASSES, H], U8, "w4_sc")
-        nc.vector.tensor_copy(w4_sc[:].rearrange("p a (b t m) -> p a b t m", b=PASSES, t=PACK),
-                              w4s_raw[:].rearrange("p a (b m t) -> p a b t m", b=PASSES, t=PACK))
+        to_planes(v_scales, picked_scales)
 
         turned = psum.tile([P, BANK], F32, name="turned", tag="h_bank")
         for c in range(4):
@@ -118,15 +123,15 @@ def tile_list_slide_dye_repair_kernel(tc, tab_words, tab_scales, offs, pos1, pos
         for c in range(4):
             nc.scalar.copy(spread[:, c],
                            turned[:, P * c : P * (c + 1)].rearrange("p (i t) -> p t i", t=PACK).unsqueeze(2).to_broadcast([P, PACK, 4, 32]))
-        weight = {}
+        weight, dealt = {}, {}
         for t in range(PACK):
-            dealt = psum.tile([P, BANK], F32, name="dealt", tag="aux_bank")
+            dealt[t] = psum.tile([P, BANK], F32, name="dealt", tag="aux_bank")
             for c in range(4):
-                nc.tensor.transpose(dealt[:, P * c : P * (c + 1)], spread[:, c, t].rearrange("p q i -> p (q i)"), ident[:])
-            for b in range(PASSES):
-                i = PACK * b + t
-                weight[i] = kept([P, NP], F32, "weight%d" % i)
-                nc.scalar.activation(weight[i][:], dealt[:], ACT.Copy, scale=rowvec["tint"][:, i : i + 1])
+                nc.tensor.transpose(dealt[t][:, P * c : P * (c + 1)], spread[:, c, t].rearrange("p q i -> p (q i)"), ident[:])
+
+        def make_weight(i):
+            weight[i] = ring.tile([P, NP], F32, name="weight", tag="weight", bufs=TILES, align_bytes=64)
+            nc.scalar.activation(weight[i][:], dealt[i % PACK][:], ACT.Copy, scale=rowvec["tint"][:, i : i + 1])
 
         v0 = kept([P, S], U32, "v0")
         nc.vector.tensor_copy(v0[:], table[0][:].bitcast(U32).indirect(idx[:]))
@@ -166,10 +171,10 @@ def tile_list_slide_dye_repair_kernel(tc, tab_words, tab_scales, offs, pos1, pos
                 nc.vector.tensor_tensor(h[i][:, cols], bank[:], dens_sb[i][:, cols], ALU.mult)
                 nc.gpsimd.tensor_scalar(page[i][:, cols], h[i][:, cols], rowvec["skip"][:, i : i + 1], 0.0, ALU.mult, ALU.add)
             nc.vector.tensor_reduce(top[:, i : i + 1], h[i][:], AX.X, ALU.max)
+            nc.vector.tensor_scalar(look_bias[:, i : i + 1], top[:, i : i + 1], rowvec["temp"][:, i : i + 1], -1.0, ALU.mult, ALU.mult)
 
         def look_at_h(i):
-            nc.scalar.activation(look_bias[:, i : i + 1], top[:, i : i + 1], ACT.Copy, scale=neg_temp[:, i : i + 1])
-            look[i] = ring.tile([P, NP], F32, name="look")
+            look[i] = ring.tile([P, NP], F32, name="look", bufs=2)
             nc.scalar.activation(look[i][:], h[i][:].indirect(p1[:]), ACT.Exp,
                                  bias=look_bias[:, i : i + 1], scale=rowvec["temp"][:, i : i + 1])
 
@@ -178,12 +183,12 @@ def tile_list_slide_dye_repair_kernel(tc, tab_words, tab_scales, offs, pos1, pos
 
         def bend(i):
             b, t = divmod(i, PACK)
-            bent[i] = ring.tile([P, S], F32, name="bent")
+            bent[i] = ring.tile([P, S], F32, name="bent", bufs=1)
             nc.scalar.activation(bent[i][:], page[i][:], ACT.Tanh)
             nc.scalar.activation(f_rows[b][:, t], bent[i][:], ACT.Copy, scale=rowvec["gain"][:, i : i + 1])
 
-        def weave(copy, rows, width):
-            woven = ring.tile([P, width, PACK], BF16, name="woven", bufs=3, align_bytes=64)
+        def weave(copy, rows, width, tag, bufs):
+            woven = ring.tile([P, width, PACK], BF16, name="woven", tag=tag, bufs=bufs, align_bytes=64)
             copy(woven[:].rearrange("p (c i) t -> p c t i", i=4), rows.rearrange("p t (c i) -> p c t i", i=4))
             return woven
 
@@ -193,58 +198,65 @@ def tile_list_slide_dye_repair_kernel(tc, tab_words, tab_scales, offs, pos1, pos
         def w2_piece(k):
             b, u = divmod(k, 2)
             cols = slice(W2_PIECE * u, W2_PIECE * (u + 1))
-            quantise(weave(nc.scalar.copy, w2_raw[b][:, :, cols], W2_PIECE), w2_codes[b][:, cols], w2_scales[b][:, cols])
+            quantise(weave(nc.scalar.copy, w2_raw[k][:], W2_PIECE, "weight", TILES), w2_codes[b][:, cols], w2_scales[b][:, cols])
 
         def f_piece(b, c, copy):
             cols = slice(CHUNK * c, CHUNK * (c + 1))
-            quantise(weave(copy, f_rows[b][:, :, cols], CHUNK), f_codes[b][:, cols], f_scales[b][:, cols])
+            quantise(weave(copy, f_rows[b][:, :, cols], CHUNK, "woven%d" % b, 4 - 3 * b), f_codes[b][:, cols], f_scales[b][:, cols])
 
-        def out_pass(bank, c, pair, b):
-            cols = slice(CHUNK * c, CHUNK * (c + 1))
-            for e in range(2):
-                rows = slice(P * (2 * pair + e), P * (2 * pair + e + 1))
+        def out_pass(bank, parts, b):
+            for e, (m, cols) in enumerate(parts):
+                rows = slice(P * m, P * (m + 1))
+                width = cols.stop - cols.start
                 nc.tensor.matmul_mx(
-                    out=bank[:, CHUNK * e : CHUNK * (e + 1)],
+                    out=bank[:, width * e : width * (e + 1)],
                     lhsT=w2_codes[b][:, rows].bitcast(FP8X4), lhsT_scale=w2_scales[b][:, rows],
                     rhs=f_codes[b][:, cols].bitcast(FP8X4), rhs_scale=f_scales[b][:, cols],
-                    start=(b == 0 and e == 0), stop=(b == PASSES - 1 and e == 1))
+                    start=(b == 0 and e == 0), stop=(b == PASSES - 1 and e == len(parts) - 1))
 
-        neg_temp = kept([P, TILES], F32, "neg_temp")
-        nc.scalar.activation(neg_temp[:], rowvec["temp"][:], ACT.Copy, scale=-1.0)
         deal_w4(0, 0, 1)
         deal_w4(0, 1, PACK)
-        make_h(0)
+        for i in range(AHEAD):
+            make_h(i)
         look_at_h(0)
         for i in range(TILES):
-            if i + 6 < TILES:
-                load_dens(i + 6)
-            if i == 1:
+            make_weight(i)
+        for i in range(TILES):
+            if i < 4:
+                load_w2(i)
+                load_dens(i + 4)
+            if i == 0:
                 deal_w4(1, 0, PACK)
+            if i + AHEAD < TILES:
+                make_h(i + AHEAD)
             if i + 1 < TILES:
-                make_h(i + 1)
                 look_at_h(i + 1)
             put(i)
             if i + 1 < TILES:
                 bend(i)
-            if i in (1, 2):
-                w2_piece(i - 1)
+            if i < 4:
+                w2_piece(i)
             if i in (3, 4):
                 f_piece(0, 2 * (i - 3), nc.scalar.copy)
                 f_piece(0, 2 * (i - 3) + 1, nc.scalar.copy)
-            if i in (5, 6):
-                w2_piece(i - 3)
 
-        out_rows = out.rearrange("(pair e p) j -> pair p e j", e=2, p=P)
+        out_rows = out.rearrange("(m p) j -> p m j", p=P)
+        plan = []
+        for c in range(2):
+            for pair in range(3):
+                plan.append((c, [(2 * pair + e, slice(CHUNK * c, CHUNK * (c + 1))) for e in range(2)]))
+        for m in range(6):
+            plan.append((3, [(m, slice(BANK, S))]))
         banks = {}
 
         def open_bank(k):
             banks[k] = psum.tile([P, BANK], F32, name="acc", tag=("aux_bank" if (k // 4) % 2 == 0 else "h_bank"))
-            out_pass(banks[k], k // 3, k % 3, 0)
+            out_pass(banks[k], plan[k][1], 0)
 
         for k in range(8):
             open_bank(k)
         last = TILES - 1
-        bent[last] = ring.tile([P, S], F32, name="bent")
+        bent[last] = ring.tile([P, S], F32, name="bent", bufs=1)
         for c in range(S // CHUNK):
             cols = slice(CHUNK * c, CHUNK * (c + 1))
             nc.scalar.activation(bent[last][:, cols], page[last][:, cols], ACT.Tanh)
@@ -252,11 +264,13 @@ def tile_list_slide_dye_repair_kernel(tc, tab_words, tab_scales, offs, pos1, pos
             cols = slice(CHUNK * c, CHUNK * (c + 1))
             nc.vector.tensor_scalar(f_rows[1][:, PACK - 1, cols], bent[last][:, cols], rowvec["gain"][:, last : last + 1], None, ALU.mult)
             f_piece(1, c, nc.vector.tensor_copy)
-            for pair in range(3):
-                k = 3 * c + pair
-                if k not in banks:
-                    open_bank(k)
-                out_pass(banks[k], c, pair, 1)
-                result = ring.tile([P, 2, CHUNK], F32, name="result", bufs=6)
-                nc.scalar.activation(result[:].rearrange("p e j -> p (e j)"), banks[k][:], ACT.Abs)
-                nc.sync.dma_start(out_rows[pair][:, :, cols], result[:])
+            for k in range(len(plan)):
+                if plan[k][0] == c:
+                    parts = plan[k][1]
+                    if k not in banks:
+                        open_bank(k)
+                    out_pass(banks[k], parts, 1)
+                    result = ring.tile([P, BANK], F32, name="result", bufs=6)
+                    nc.scalar.activation(result[:], banks[k][:], ACT.Abs)
+                    nc.sync.dma_start(out_rows[:, parts[0][0] : parts[-1][0] + 1, parts[0][1]],
+                                      result[:].rearrange("p (e j) -> p e j", e=len(parts)))

@@ -23,7 +23,7 @@ PACK = 4
 PASSES = 2
 TILES = PASSES * PACK
 BANK = 512
-CHUNK = 256
+EDGES = (0, 256, 512, 1024)
 W2_PIECE = 384
 AHEAD = 2
 
@@ -41,8 +41,12 @@ def tile_list_slide_dye_repair_kernel(tc, tab_words, tab_scales, offs, pos1, pos
 
         idx = keep.tile([P, S // 16], U16, name="idx")
         nc.sync.dma_start(idx[:], offs)
+        p1 = keep.tile([P, NP // 16], U16, name="p1")
+        nc.sync.dma_start(p1[:], pos1)
+        p2 = keep.tile([P, NP // 16], U16, name="p2")
+        nc.sync.dma_start(p2[:], pos2)
         table_scales = kept([P, T], U8, "table_scales")
-        w4s_raw = kept([P, H], U8, "w4s_raw")
+        w4s_raw = ring.tile([P, H], U8, name="w4s_raw", tag="second_table", bufs=1, align_bytes=64)
         nc.sync.dma_start(w4s_raw[0:32, :].bitcast(I32), w4_scales.rearrange("a r c -> r a c").bitcast(I32))
         nc.sync.dma_start(table_scales[0:32, :].bitcast(I32), tab_scales.rearrange("a r t -> r a t").bitcast(I32))
         wgs_rows = kept([P, NP], F32, "wgs_rows")
@@ -55,9 +59,13 @@ def tile_list_slide_dye_repair_kernel(tc, tab_words, tab_scales, offs, pos1, pos
                             vec.rearrange("(b p t) -> p b t", p=P, t=PACK))
 
         load_rowvec(nc.sync, "tint", tint)
-        table = [kept([P, T], I32, "table%d" % a) for a in range(PASSES)]
-        for a in range(PASSES):
-            nc.sync.dma_start(table[a][:], tab_words[a].rearrange("p t i -> p (t i)").bitcast(I32))
+        table = {}
+
+        def load_table(a, tile):
+            table[a] = tile
+            nc.sync.dma_start(tile[:], tab_words[a].rearrange("p t i -> p (t i)").bitcast(I32))
+
+        load_table(0, ring.tile([P, T], I32, name="table0", tag="first_table", bufs=1, align_bytes=64))
 
         ident = kept([P, P], F32, "ident")
         make_identity(nc, ident[:])
@@ -71,16 +79,20 @@ def tile_list_slide_dye_repair_kernel(tc, tab_words, tab_scales, offs, pos1, pos
 
         def to_planes(planes, rows):
             for q in range(4):
-                nc.gpsimd.dma_start(planes[32 * q : 32 * q + 4].bitcast(I32), rows[8 * q : 8 * q + 8, :].bitcast(I32))
+                nc.sync.dma_start(planes[32 * q : 32 * q + 4].bitcast(I32), rows[8 * q : 8 * q + 8, :].bitcast(I32))
 
         w4s_dealt = kept([P, H], U8, "w4s_dealt")
         nc.vector.tensor_copy(w4s_dealt[:].rearrange("p (b t m) -> p b t m", b=PASSES, t=PACK),
                               w4s_raw[:].rearrange("p (b m t) -> p b t m", b=PASSES, t=PACK))
         to_planes(w4_sc, w4s_dealt)
+        load_table(1, ring.tile([P, T], I32, name="table1", tag="second_table", bufs=1, align_bytes=64))
+        for name, vec in (("temp", temp), ("skip", skip), ("gain", gain)):
+            load_rowvec(nc.gpsimd, name, vec)
 
-        w4_raw = [kept([P, PASSES, BANK], U16, "w4_raw%d" % b) for b in range(PASSES)]
+        w4_raw = {}
 
         def load_w4(b):
+            w4_raw[b] = ring.tile([P, PASSES, BANK], U16, name="w4_raw", tag="stream", bufs=4)
             nc.sync.dma_start(w4_raw[b][:].bitcast(I32),
                               w4_words[:, :, 2 * BANK * b : 2 * BANK * (b + 1)].rearrange("a p c -> p a c").bitcast(I32))
 
@@ -88,29 +100,15 @@ def tile_list_slide_dye_repair_kernel(tc, tab_words, tab_scales, offs, pos1, pos
         dens_sb = {}
 
         def load_dens(i):
-            dens_sb[i] = ring.tile([P, S], F32, name="dens_sb", tag="stream", bufs=5)
+            dens_sb[i] = ring.tile([P, S], F32, name="dens_sb", tag="stream", bufs=4)
             nc.sync.dma_start(dens_sb[i][:], dens_rows[i // PACK, i % PACK])
 
-        load_w4(0)
-        load_dens(0)
-        p1 = keep.tile([P, NP // 16], U16, name="p1")
-        nc.sync.dma_start(p1[:], pos1)
-        p2 = keep.tile([P, NP // 16], U16, name="p2")
-        nc.sync.dma_start(p2[:], pos2)
-        load_rowvec(nc.sync, "temp", temp)
-        load_rowvec(nc.sync, "skip", skip)
-        load_rowvec(nc.sync, "gain", gain)
-        load_dens(1)
-        load_dens(2)
-        load_w4(1)
-        load_dens(3)
         w2_raw = {}
         w2_rows = w2.rearrange("(b p t) n -> b p t n", p=P, t=PACK)
 
-        def load_w2(k):
-            b, u = divmod(k, 2)
-            w2_raw[k] = ring.tile([P, PACK, W2_PIECE], F32, name="w2_raw", tag="stream", bufs=5)
-            nc.sync.dma_start(w2_raw[k][:], w2_rows[b][:, :, W2_PIECE * u : W2_PIECE * (u + 1)])
+        def load_w2(b):
+            w2_raw[b] = ring.tile([P, PACK, N], F32, name="w2_raw", tag=("first_table", "second_table")[b], bufs=1, align_bytes=64)
+            nc.sync.dma_start(w2_raw[b][:], w2_rows[b])
 
         picked_scales = kept([P, S], U8, "picked_scales")
         nc.vector.tensor_copy(picked_scales[:], table_scales[:].indirect(idx[:]))
@@ -119,15 +117,21 @@ def tile_list_slide_dye_repair_kernel(tc, tab_words, tab_scales, offs, pos1, pos
         turned = psum.tile([P, BANK], F32, name="turned", tag="h_bank")
         for c in range(4):
             nc.tensor.transpose(turned[:, P * c : P * (c + 1)], wgs_rows[:, P * c : P * (c + 1)], ident[:])
-        spread = kept([P, 4, PACK, 4, 32], F32, "spread")
+        spread = [ring.tile([P, PACK, 4, 32], F32, name="spread", tag="stream", bufs=4) for c in range(4)]
         for c in range(4):
-            nc.scalar.copy(spread[:, c],
+            nc.scalar.copy(spread[c][:],
                            turned[:, P * c : P * (c + 1)].rearrange("p (i t) -> p t i", t=PACK).unsqueeze(2).to_broadcast([P, PACK, 4, 32]))
         weight, dealt = {}, {}
         for t in range(PACK):
             dealt[t] = psum.tile([P, BANK], F32, name="dealt", tag="aux_bank")
             for c in range(4):
-                nc.tensor.transpose(dealt[t][:, P * c : P * (c + 1)], spread[:, c, t].rearrange("p q i -> p (q i)"), ident[:])
+                nc.tensor.transpose(dealt[t][:, P * c : P * (c + 1)], spread[c][:, t].rearrange("p q i -> p (q i)"), ident[:])
+        load_w4(0)
+        load_dens(0)
+        load_dens(1)
+        load_dens(2)
+        load_w4(1)
+        load_dens(3)
 
         def make_weight(i):
             weight[i] = ring.tile([P, NP], F32, name="weight", tag="weight", bufs=TILES, align_bytes=64)
@@ -169,7 +173,7 @@ def tile_list_slide_dye_repair_kernel(tc, tab_words, tab_scales, offs, pos1, pos
                         rhs_scale=v_scales[:, a, cols],
                         start=(a == 0), stop=(a == PASSES - 1))
                 nc.vector.tensor_tensor(h[i][:, cols], bank[:], dens_sb[i][:, cols], ALU.mult)
-                nc.gpsimd.tensor_scalar(page[i][:, cols], h[i][:, cols], rowvec["skip"][:, i : i + 1], 0.0, ALU.mult, ALU.add)
+            nc.gpsimd.tensor_scalar(page[i][:], h[i][:], rowvec["skip"][:, i : i + 1], 0.0, ALU.mult, ALU.add)
             nc.vector.tensor_reduce(top[:, i : i + 1], h[i][:], AX.X, ALU.max)
             nc.vector.tensor_scalar(look_bias[:, i : i + 1], top[:, i : i + 1], rowvec["temp"][:, i : i + 1], -1.0, ALU.mult, ALU.mult)
 
@@ -198,11 +202,10 @@ def tile_list_slide_dye_repair_kernel(tc, tab_words, tab_scales, offs, pos1, pos
         def w2_piece(k):
             b, u = divmod(k, 2)
             cols = slice(W2_PIECE * u, W2_PIECE * (u + 1))
-            quantise(weave(nc.scalar.copy, w2_raw[k][:], W2_PIECE, "weight", TILES), w2_codes[b][:, cols], w2_scales[b][:, cols])
+            quantise(weave(nc.scalar.copy, w2_raw[b][:, :, cols], W2_PIECE, "weight", TILES), w2_codes[b][:, cols], w2_scales[b][:, cols])
 
-        def f_piece(b, c, copy):
-            cols = slice(CHUNK * c, CHUNK * (c + 1))
-            quantise(weave(copy, f_rows[b][:, :, cols], CHUNK, "woven%d" % b, 4 - 3 * b), f_codes[b][:, cols], f_scales[b][:, cols])
+        def f_piece(b, cols, copy):
+            quantise(weave(copy, f_rows[b][:, :, cols], cols.stop - cols.start, "woven%d" % b, 2 - b), f_codes[b][:, cols], f_scales[b][:, cols])
 
         def out_pass(bank, parts, b):
             for e, (m, cols) in enumerate(parts):
@@ -223,8 +226,9 @@ def tile_list_slide_dye_repair_kernel(tc, tab_words, tab_scales, offs, pos1, pos
             make_weight(i)
         for i in range(TILES):
             if i < 4:
-                load_w2(i)
                 load_dens(i + 4)
+            if i < PASSES:
+                load_w2(i)
             if i == 0:
                 deal_w4(1, 0, PACK)
             if i + AHEAD < TILES:
@@ -237,16 +241,15 @@ def tile_list_slide_dye_repair_kernel(tc, tab_words, tab_scales, offs, pos1, pos
             if i < 4:
                 w2_piece(i)
             if i in (3, 4):
-                f_piece(0, 2 * (i - 3), nc.scalar.copy)
-                f_piece(0, 2 * (i - 3) + 1, nc.scalar.copy)
+                f_piece(0, slice(BANK * (i - 3), BANK * (i - 2)), nc.scalar.copy)
 
         out_rows = out.rearrange("(m p) j -> p m j", p=P)
+        chunks = [slice(EDGES[c], EDGES[c + 1]) for c in range(len(EDGES) - 1)]
         plan = []
-        for c in range(2):
-            for pair in range(3):
-                plan.append((c, [(2 * pair + e, slice(CHUNK * c, CHUNK * (c + 1))) for e in range(2)]))
-        for m in range(6):
-            plan.append((3, [(m, slice(BANK, S))]))
+        for c, cols in enumerate(chunks):
+            per_bank = min(BANK // (cols.stop - cols.start), 3)
+            for m in range(0, N // P, per_bank):
+                plan.append((c, [(m + e, cols) for e in range(per_bank)]))
         banks = {}
 
         def open_bank(k):
@@ -257,20 +260,19 @@ def tile_list_slide_dye_repair_kernel(tc, tab_words, tab_scales, offs, pos1, pos
             open_bank(k)
         last = TILES - 1
         bent[last] = ring.tile([P, S], F32, name="bent", bufs=1)
-        for c in range(S // CHUNK):
-            cols = slice(CHUNK * c, CHUNK * (c + 1))
+        for cols in chunks:
             nc.scalar.activation(bent[last][:, cols], page[last][:, cols], ACT.Tanh)
-        for c in range(S // CHUNK):
-            cols = slice(CHUNK * c, CHUNK * (c + 1))
+        for c, cols in enumerate(chunks):
             nc.vector.tensor_scalar(f_rows[1][:, PACK - 1, cols], bent[last][:, cols], rowvec["gain"][:, last : last + 1], None, ALU.mult)
-            f_piece(1, c, nc.vector.tensor_copy)
+            f_piece(1, cols, nc.vector.tensor_copy)
             for k in range(len(plan)):
                 if plan[k][0] == c:
                     parts = plan[k][1]
                     if k not in banks:
                         open_bank(k)
                     out_pass(banks[k], parts, 1)
-                    result = ring.tile([P, BANK], F32, name="result", bufs=6)
-                    nc.scalar.activation(result[:], banks[k][:], ACT.Abs)
+                    used = len(parts) * (cols.stop - cols.start)
+                    result = ring.tile([P, used], F32, name="result", bufs=8)
+                    nc.scalar.activation(result[:], banks[k][:, 0:used], ACT.Abs)
                     nc.sync.dma_start(out_rows[:, parts[0][0] : parts[-1][0] + 1, parts[0][1]],
                                       result[:].rearrange("p (e j) -> p e j", e=len(parts)))

from contextlib import ExitStack

import concourse.mybir as mybir
from concourse.masks import make_identity

K, T, S, NP, H, N = 1024, 4096, 1024, 512, 1024, 768
FLOPS = 2 * K * H * S + 2 * H * N * S

F32 = mybir.dt.float32
BF16 = mybir.dt.bfloat16
I32 = mybir.dt.int32
U32 = mybir.dt.uint32
U16 = mybir.dt.uint16
U8 = mybir.dt.uint8
FP8X4 = mybir.dt.float8_e4m3fn_x4
FP4X4 = mybir.dt.float4_e2m1fn_x4
ACT = mybir.ActivationFunctionType
ALU = mybir.AluOpType
AX = mybir.AxisListType

P = 128
PACK = 4
PASSES = 2
TILES = PASSES * PACK
BANK = 512
EDGES = (0, 256, 512, 1024)
W2_PIECE = 384
AHEAD = 2


def tile_list_slide_dye_repair_kernel(tc, tab_words, tab_scales, offs, pos1, pos2, w4_words, w4_scales,
                                                dens, temp, tint, skip, wgs, gain, w2, out):
    nc = tc.nc
    with ExitStack() as ctx:
        keep = ctx.enter_context(tc.tile_pool(name="keep", bufs=1))
        ring = ctx.enter_context(tc.tile_pool(name="ring", bufs=2))
        psum = ctx.enter_context(tc.psum_pool(name="psum", bufs=4))

        def kept(shape, dtype, name):
            return keep.tile(shape, dtype, name=name, align_bytes=64)

        idx = keep.tile([P, S // 16], U16, name="idx")
        nc.sync.dma_start(idx[:], offs)
        p1 = keep.tile([P, NP // 16], U16, name="p1")
        nc.sync.dma_start(p1[:], pos1)
        p2 = keep.tile([P, NP // 16], U16, name="p2")
        nc.sync.dma_start(p2[:], pos2)
        table_scales = kept([P, T], U8, "table_scales")
        w4s_raw = ring.tile([P, H], U8, name="w4s_raw", tag="second_table", bufs=1, align_bytes=64)
        nc.sync.dma_start(w4s_raw[0:32, :].bitcast(I32), w4_scales.rearrange("a r c -> r a c").bitcast(I32))
        nc.sync.dma_start(table_scales[0:32, :].bitcast(I32), tab_scales.rearrange("a r t -> r a t").bitcast(I32))
        wgs_rows = kept([P, NP], F32, "wgs_rows")
        nc.sync.dma_start(wgs_rows[:], wgs)
        rowvec = {}

        def load_rowvec(queue, name, vec):
            rowvec[name] = kept([P, TILES], F32, name + "_rows")
            queue.dma_start(rowvec[name][:].rearrange("p (b t) -> p b t", t=PACK),
                            vec.rearrange("(b p t) -> p b t", p=P, t=PACK))

        load_rowvec(nc.sync, "tint", tint)
        table = {}

        def load_table(a, tile):
            table[a] = tile
            nc.sync.dma_start(tile[:], tab_words[a].rearrange("p t i -> p (t i)").bitcast(I32))

        load_table(0, ring.tile([P, T], I32, name="table0", tag="first_table", bufs=1, align_bytes=64))

        ident = kept([P, P], F32, "ident")
        make_identity(nc, ident[:])
        for rows in (w4s_raw, table_scales):
            nc.vector.memset(rows[32:64, :].bitcast(I32), 0)
            nc.vector.memset(rows[64:P, :].bitcast(I32), 0)
        w4_sc = kept([P, PASSES, H], U8, "w4_sc")
        v_scales = kept([P, PASSES, S], U8, "v_scales")
        for plane in (w4_sc, v_scales):
            nc.gpsimd.memset(plane[:].bitcast(I32), 0)

        def to_planes(planes, rows):
            for q in range(4):
                nc.sync.dma_start(planes[32 * q : 32 * q + 4].bitcast(I32), rows[8 * q : 8 * q + 8, :].bitcast(I32))

        w4s_dealt = kept([P, H], U8, "w4s_dealt")
        nc.vector.tensor_copy(w4s_dealt[:].rearrange("p (b t m) -> p b t m", b=PASSES, t=PACK),
                              w4s_raw[:].rearrange("p (b m t) -> p b t m", b=PASSES, t=PACK))
        to_planes(w4_sc, w4s_dealt)
        load_table(1, ring.tile([P, T], I32, name="table1", tag="second_table", bufs=1, align_bytes=64))
        for name, vec in (("temp", temp), ("skip", skip), ("gain", gain)):
            load_rowvec(nc.gpsimd, name, vec)

        w4_raw = {}

        def load_w4(b):
            w4_raw[b] = ring.tile([P, PASSES, BANK], U16, name="w4_raw", tag="stream", bufs=4)
            nc.sync.dma_start(w4_raw[b][:].bitcast(I32),
                              w4_words[:, :, 2 * BANK * b : 2 * BANK * (b + 1)].rearrange("a p c -> p a c").bitcast(I32))

        dens_rows = dens.rearrange("(b p t) j -> b t p j", p=P, t=PACK)
        dens_sb = {}

        def load_dens(i):
            dens_sb[i] = ring.tile([P, S], F32, name="dens_sb", tag="stream", bufs=4)
            nc.sync.dma_start(dens_sb[i][:], dens_rows[i // PACK, i % PACK])

        w2_raw = {}
        w2_rows = w2.rearrange("(b p t) n -> b p t n", p=P, t=PACK)

        def load_w2(b):
            w2_raw[b] = ring.tile([P, PACK, N], F32, name="w2_raw", tag=("first_table", "second_table")[b], bufs=1, align_bytes=64)
            nc.sync.dma_start(w2_raw[b][:], w2_rows[b])

        picked_scales = kept([P, S], U8, "picked_scales")
        nc.vector.tensor_copy(picked_scales[:], table_scales[:].indirect(idx[:]))
        to_planes(v_scales, picked_scales)

        turned = psum.tile([P, BANK], F32, name="turned", tag="h_bank")
        for c in range(4):
            nc.tensor.transpose(turned[:, P * c : P * (c + 1)], wgs_rows[:, P * c : P * (c + 1)], ident[:])
        spread = [ring.tile([P, PACK, 4, 32], F32, name="spread", tag="stream", bufs=4) for c in range(4)]
        for c in range(4):
            nc.scalar.copy(spread[c][:],
                           turned[:, P * c : P * (c + 1)].rearrange("p (i t) -> p t i", t=PACK).unsqueeze(2).to_broadcast([P, PACK, 4, 32]))
        weight, dealt = {}, {}
        for t in range(PACK):
            dealt[t] = psum.tile([P, BANK], F32, name="dealt", tag="aux_bank")
            for c in range(4):
                nc.tensor.transpose(dealt[t][:, P * c : P * (c + 1)], spread[c][:, t].rearrange("p q i -> p (q i)"), ident[:])
        load_w4(0)
        load_dens(0)
        load_dens(1)
        load_dens(2)
        load_w4(1)
        load_dens(3)

        def make_weight(i):
            weight[i] = ring.tile([P, NP], F32, name="weight", tag="weight", bufs=TILES, align_bytes=64)
            nc.scalar.activation(weight[i][:], dealt[i % PACK][:], ACT.Copy, scale=rowvec["tint"][:, i : i + 1])

        v0 = kept([P, S], U32, "v0")
        nc.vector.tensor_copy(v0[:], table[0][:].bitcast(U32).indirect(idx[:]))
        v1 = [kept([P, BANK], U32, "v1_%d" % u) for u in range(2)]
        for u in range(2):
            nc.vector.tensor_copy(v1[u][:], table[1][:].bitcast(U32).indirect(idx[:, 32 * u : 32 * (u + 1)]))
        w4_w = [kept([P, PASSES, BANK], U16, "w4_w%d" % b) for b in range(PASSES)]

        def deal_w4(b, t0, t1):
            nc.scalar.copy(w4_w[b][:].rearrange("p a (t m) -> p a t m", t=PACK)[:, :, t0:t1],
                           w4_raw[b][:].rearrange("p a (m t) -> p a t m", t=PACK)[:, :, t0:t1])

        top = kept([P, TILES], F32, "top")
        look_bias = kept([P, TILES], F32, "look_bias")
        h, page, look, bent = {}, {}, {}, {}
        f_rows = [ring.tile([P, PACK, S], BF16, name="f_rows") for b in range(PASSES)]
        f_codes = [kept([P, S], U32, "f_codes%d" % b) for b in range(PASSES)]
        f_scales = [kept([P, S], U8, "f_scales%d" % b) for b in range(PASSES)]
        w2_codes = [kept([P, N], U32, "w2_codes%d" % b) for b in range(PASSES)]
        w2_scales = [kept([P, N], U8, "w2_scales%d" % b) for b in range(PASSES)]

        def make_h(i):
            b, t = divmod(i, PACK)
            h[i] = ring.tile([P, S], F32, name="h", bufs=3)
            page[i] = ring.tile([P, S], F32, name="page", bufs=3)
            for u in range(2):
                cols = slice(BANK * u, BANK * (u + 1))
                bank = psum.tile([P, BANK], F32, name="bank", tag="h_bank")
                for a in range(PASSES):
                    nc.tensor.matmul_mx(
                        out=bank[:],
                        lhsT=w4_w[b][:, a, P * t : P * (t + 1)].bitcast(FP4X4),
                        lhsT_scale=w4_sc[:, a, P * i : P * (i + 1)],
                        rhs=(v0[:, cols] if a == 0 else v1[u][:]).bitcast(FP8X4),
                        rhs_scale=v_scales[:, a, cols],
                        start=(a == 0), stop=(a == PASSES - 1))
                nc.vector.tensor_tensor(h[i][:, cols], bank[:], dens_sb[i][:, cols], ALU.mult)
            nc.gpsimd.tensor_scalar(page[i][:], h[i][:], rowvec["skip"][:, i : i + 1], 0.0, ALU.mult, ALU.add)
            nc.vector.tensor_reduce(top[:, i : i + 1], h[i][:], AX.X, ALU.max)
            nc.vector.tensor_scalar(look_bias[:, i : i + 1], top[:, i : i + 1], rowvec["temp"][:, i : i + 1], -1.0, ALU.mult, ALU.mult)

        def look_at_h(i):
            look[i] = ring.tile([P, NP], F32, name="look", bufs=2)
            nc.scalar.activation(look[i][:], h[i][:].indirect(p1[:]), ACT.Exp,
                                 bias=look_bias[:, i : i + 1], scale=rowvec["temp"][:, i : i + 1])

        def put(i):
            nc.vector.tensor_tensor(page[i][:].indirect(p2[:]), look[i][:], weight[i][:], ALU.mult)

        def bend(i):
            b, t = divmod(i, PACK)
            bent[i] = ring.tile([P, S], F32, name="bent", bufs=1)
            nc.scalar.activation(bent[i][:], page[i][:], ACT.Tanh)
            nc.scalar.activation(f_rows[b][:, t], bent[i][:], ACT.Copy, scale=rowvec["gain"][:, i : i + 1])

        def weave(copy, rows, width, tag, bufs):
            woven = ring.tile([P, width, PACK], BF16, name="woven", tag=tag, bufs=bufs, align_bytes=64)
            copy(woven[:].rearrange("p (c i) t -> p c t i", i=4), rows.rearrange("p t (c i) -> p c t i", i=4))
            return woven

        def quantise(woven, codes, scales):
            nc.vector.quantize_mx(out=codes.bitcast(FP8X4), scales=scales, in_=woven[:].rearrange("p w t -> p (w t)"))

        def w2_piece(k):
            b, u = divmod(k, 2)
            cols = slice(W2_PIECE * u, W2_PIECE * (u + 1))
            quantise(weave(nc.scalar.copy, w2_raw[b][:, :, cols], W2_PIECE, "weight", TILES), w2_codes[b][:, cols], w2_scales[b][:, cols])

        def f_piece(b, cols, copy):
            quantise(weave(copy, f_rows[b][:, :, cols], cols.stop - cols.start, "woven%d" % b, 2 - b), f_codes[b][:, cols], f_scales[b][:, cols])

        def out_pass(bank, parts, b):
            for e, (m, cols) in enumerate(parts):
                rows = slice(P * m, P * (m + 1))
                width = cols.stop - cols.start
                nc.tensor.matmul_mx(
                    out=bank[:, width * e : width * (e + 1)],
                    lhsT=w2_codes[b][:, rows].bitcast(FP8X4), lhsT_scale=w2_scales[b][:, rows],
                    rhs=f_codes[b][:, cols].bitcast(FP8X4), rhs_scale=f_scales[b][:, cols],
                    start=(b == 0 and e == 0), stop=(b == PASSES - 1 and e == len(parts) - 1))

        deal_w4(0, 0, 1)
        deal_w4(0, 1, PACK)
        for i in range(AHEAD):
            make_h(i)
        look_at_h(0)
        for i in range(TILES):
            make_weight(i)
        for i in range(TILES):
            if i < 4:
                load_dens(i + 4)
            if i < PASSES:
                load_w2(i)
            if i == 0:
                deal_w4(1, 0, PACK)
            if i + AHEAD < TILES:
                make_h(i + AHEAD)
            if i + 1 < TILES:
                look_at_h(i + 1)
            put(i)
            if i + 1 < TILES:
                bend(i)
            if i < 4:
                w2_piece(i)
            if i in (3, 4):
                f_piece(0, slice(BANK * (i - 3), BANK * (i - 2)), nc.scalar.copy)

        out_rows = out.rearrange("(m p) j -> p m j", p=P)
        chunks = [slice(EDGES[c], EDGES[c + 1]) for c in range(len(EDGES) - 1)]
        plan = []
        for c, cols in enumerate(chunks):
            per_bank = min(BANK // (cols.stop - cols.start), 3)
            for m in range(0, N // P, per_bank):
                plan.append((c, [(m + e, cols) for e in range(per_bank)]))
        banks = {}

        def open_bank(k):
            banks[k] = psum.tile([P, BANK], F32, name="acc", tag=("aux_bank" if (k // 4) % 2 == 0 else "h_bank"))
            out_pass(banks[k], plan[k][1], 0)

        for k in range(8):
            open_bank(k)
        last = TILES - 1
        bent[last] = ring.tile([P, S], F32, name="bent", bufs=1)
        for cols in chunks:
            nc.scalar.activation(bent[last][:, cols], page[last][:, cols], ACT.Tanh)
        for c, cols in enumerate(chunks):
            nc.vector.tensor_scalar(f_rows[1][:, PACK - 1, cols], bent[last][:, cols], rowvec["gain"][:, last : last + 1], None, ALU.mult)
            f_piece(1, cols, nc.vector.tensor_copy)
            for k in range(len(plan)):
                if plan[k][0] == c:
                    parts = plan[k][1]
                    if k not in banks:
                        open_bank(k)
                    out_pass(banks[k], parts, 1)
                    used = len(parts) * (cols.stop - cols.start)
                    result = ring.tile([P, used], F32, name="result", bufs=8)
                    nc.scalar.activation(result[:], banks[k][:, 0:used], ACT.Abs)
                    nc.sync.dma_start(out_rows[:, parts[0][0] : parts[-1][0] + 1, parts[0][1]],
                                      result[:].rearrange("p (e j) -> p e j", e=len(parts)))
